import numpy as np
import ml_dtypes


def mxq(x, axis, fmt="e4m3"):
    dtype, down = {"e4m3": (ml_dtypes.float8_e4m3fn, 7), "e5m2": (ml_dtypes.float8_e5m2, 14)}[fmt]
    v = np.moveaxis(np.asarray(x, np.float32).astype(ml_dtypes.bfloat16).astype(np.float64), axis, -1)
    blocks = v.reshape(v.shape[:-1] + (-1, 32))
    amax = np.abs(blocks).max(-1, keepdims=True)
    byte = np.maximum(np.where(amax > 0, np.frexp(amax)[1] - 1 + 127, 0) - down, 1)
    scale = np.exp2(byte - 127.0)
    codes = (blocks / scale).astype(np.float32).astype(dtype).astype(np.float64)
    return np.moveaxis((codes * scale).reshape(v.shape), -1, axis)


WIDE = False


def mx_kscale(k, group=512):
    if not WIDE:
        return np.ones(k)
    levels = np.array([10, -10, 5, -5, 0])
    if group != 512:
        return np.exp2(np.random.permutation(np.resize(levels, k // group))).repeat(group)
    if k % 512:
        return np.exp2(np.random.permutation(np.resize(levels, k // 32))).repeat(32)
    a = np.empty((k // 512, 16))
    for p in range(k // 512):
        a[p, :8] = np.random.permutation(np.resize(levels, 8))
        for g in range(8):
            far = levels[np.abs(levels - a[p, g]) >= 10]
            a[p, g + 8] = far[np.random.randint(len(far))]
    return np.exp2(a.ravel()).repeat(32)


def f64(x):
    return np.asarray(x).astype(np.float64)


def striped(idx):
    return np.tile(np.asarray(idx).reshape(-1, 16).T, (8, 1)).astype(np.uint16)


def unstriped(offs):
    return offs[:16].T.reshape(-1).astype(np.int64)


H, KV, D, NQ, N = 4, 4, 128, 512, 1024


def setup_inputs():
    n = np.random.standard_normal
    s = mx_kscale(D, 0)[:, None]
    u = mx_kscale(N)
    t = np.random.uniform(0.5, 2.0, N) * u
    v = n((KV, N, 128))
    v[:, :, 127] = 1.0
    return {
        "qT": (n((H, D, NQ)) * s * (0.70 / np.sqrt(D))).astype(np.float32),
        "kT": (n((KV, D, N)) / s).astype(np.float32),
        "t": t.reshape(N, 1).astype(np.float32),
        "v": (v / t[:, None]).astype(np.float32),
        "mask": (np.arange(N)[:, None] <= np.sort(np.random.randint(N // 4, N, NQ))[None, :]).astype(np.float32),
    }


def reference(qT, kT, t, v, mask):
    a = mxq(f64(kT), 1, "e4m3").transpose(0, 2, 1) @ mxq(f64(qT), 1, "e4m3")
    p = np.square(np.maximum(a, 0.0))
    p = p * f64(mask)
    w = p * f64(t)
    y = mxq(w, 1, "e4m3").transpose(0, 2, 1) @ mxq(f64(v), 1, "e4m3")
    y = y / (y[:, :, 127:128] + 1.0)
    return y

@@ -1,0 +1,392 @@
+from contextlib import ExitStack
+
+import concourse.mybir as mybir
+
+H, D, NQ, N = 4, 128, 512, 1024
+FLOPS = 2 * 2 * H * N * NQ * D
+
+F32 = mybir.dt.float32
+BF16 = mybir.dt.bfloat16
+U32 = mybir.dt.uint32
+U8 = mybir.dt.uint8
+FP8X4 = mybir.dt.float8_e4m3fn_x4
+ALU = mybir.AluOpType
+ACT = mybir.ActivationFunctionType
+
+P = 128
+PACK = 4
+ROWS = D // PACK
+PASS = P * PACK
+PASSES = N // PASS
+QT = 128
+QTILES = NQ // QT
+STEPS = PASSES * QTILES
+K_SPLIT = 84
+
+
+def tile_rows_a_relu2_mask_kernel(tc, qT, kT, t, v, mask, out):
+    nc = tc.nc
+    with ExitStack() as ctx:
+        sb = ctx.enter_context(tc.tile_pool(name="sb", bufs=1))
+        ps = ctx.enter_context(tc.psum_pool(name="ps", bufs=1))
+        ctx.enter_context(tc.manual_schedule())
+
+        def tile(name, shape, dtype):
+            return sb.tile(shape, dtype, name=name, align_bytes=64)
+
+        t_sb = tile("t_sb", [P, PASSES, PACK], F32)
+        t_abs = tile("t_abs", [P, PASSES, PACK], F32)
+        t_pos = tile("t_pos", [P, PASSES, PACK], F32)
+        t_sign = tile("t_sign", [P, PASSES, PACK], F32)
+        guess = tile("guess", [P, PASSES, PACK], F32)
+        inv_guess = tile("inv_guess", [P, PASSES, PACK], F32)
+        half_quot = tile("half_quot", [P, PASSES, PACK], F32)
+        t_root = tile("t_root", [P, PASSES, PACK], F32)
+
+        k_raw = [tile("k_raw%d" % c, [P, PACK, PASS], F32) for c in range(PASSES)]
+        k_bf = [tile("k_bf%d" % c, [P, PACK, P, PACK], BF16) for c in range(PASSES)]
+        k_codes = [tile("k_codes%d" % c, [P, PASS], U32) for c in range(PASSES)]
+        k_scales = [tile("k_scales%d" % c, [P, PASS], U8) for c in range(PASSES)]
+        q_parts = [(0, 1), (1, 2), (2, 4)]
+        q_raw = [tile("q_raw%d" % i, [P, PACK, (b - a) * QT], F32) for i, (a, b) in enumerate(q_parts)]
+        q_bf = [tile("q_bf%d" % i, [P, (b - a) * QT, PACK], BF16) for i, (a, b) in enumerate(q_parts)]
+        q_codes = [tile("q_codes%d" % i, [P, (b - a) * QT], U32) for i, (a, b) in enumerate(q_parts)]
+        q_scales = [tile("q_scales%d" % i, [P, (b - a) * QT], U8) for i, (a, b) in enumerate(q_parts)]
+        m0a = tile("m0a", [P, PACK, 2 * QT], F32)
+        m0b = tile("m0b", [P, PACK, 2 * QT], F32)
+        m1a = tile("m1a", [P, PACK, 2 * QT], F32)
+        m1b = tile("m1b", [P, PACK, 2 * QT], F32)
+        v_raw = {(c, h0): tile("v_raw%d_%d" % (c, h0), [P, 2, PACK, D], F32) for c in range(PASSES) for h0 in (0, 2)}
+        v_bf = tile("v_bf", [P, 2, D, PACK], BF16)
+        v_codes = [tile("v_codes%d" % c, [P, H * D], U32) for c in range(PASSES)]
+        v_scales = [tile("v_scales%d" % c, [P, H * D], U8) for c in range(PASSES)]
+
+        score = [ps.tile([P, PACK, QT], F32, name="score%d" % h) for h in range(H)]
+        ybank = [ps.tile([P, H, D], F32, name="ybank%d" % i) for i in range(QTILES)]
+
+        def groups(n):
+            return [(0, 2), (2, 4)] if n < STEPS - 1 else [(0, 1), (1, 2), (2, 3), (3, 4)]
+
+        def units(n):
+            return [(0, 4)] if n < STEPS - 1 else [(0, 2), (2, 3), (3, 4)]
+
+        roots = {}
+        w_bf = {}
+        w_codes = {}
+        w_scales = {}
+        for n in range(STEPS):
+            for a, b in groups(n):
+                roots[n, a] = tile("roots%d_%d" % (n, a), [P, PACK, (b - a) * QT], F32)
+            for a, b in units(n):
+                w_bf[n, a] = tile("w_bf%d_%d" % (n, a), [P, (b - a) * QT, PACK], BF16)
+                w_codes[n, a] = tile("w_codes%d_%d" % (n, a), [P, (b - a) * QT], U32)
+                w_scales[n, a] = tile("w_scales%d_%d" % (n, a), [P, (b - a) * QT], U8)
+
+        def holder(spans, h):
+            return [a for a, b in spans if a <= h < b][0]
+
+        k_view = kT.rearrange("h (p j) n -> (h p) j n", j=PACK)
+        q_view = qT.rearrange("h (p j) n -> (h p) j n", j=PACK)
+        m_view = mask.rearrange("(c p j) q -> c p j q", c=PASSES, j=PACK)
+        v_view = v.rearrange("h (c p j) e -> c p h (j e)", c=PASSES, j=PACK)
+        nc.sync.dma_start(out=t_sb[:], in_=t.rearrange("(c p j) o -> p c (j o)", c=PASSES, j=PACK))
+        nc.sync.dma_start(out=k_raw[0][:], in_=k_view[:, :, 0:PASS])
+        nc.sync.dma_start(out=q_raw[0][:], in_=q_view[:, :, 0:QT])
+        nc.sync.dma_start(out=m0a[:], in_=m_view[0][:, :, 0 : 2 * QT])
+        nc.sync.dma_start(out=q_raw[1][:], in_=q_view[:, :, QT : 2 * QT])
+
+        def load_v(c, h0):
+            nc.sync.dma_start(out=v_raw[c, h0][:].rearrange("p h j e -> p h (j e)"), in_=v_view[c][:, h0 : h0 + 2, :])
+
+        nc.sync.dma_start(out=q_raw[2][:], in_=q_view[:, :, 2 * QT : NQ])
+        nc.sync.dma_start(out=m0b[:], in_=m_view[0][:, :, 2 * QT : NQ])
+        load_v(0, 0)
+        load_v(0, 2)
+        nc.sync.dma_start(out=k_raw[1][:], in_=k_view[:, :, PASS:N])
+        nc.sync.dma_start(out=m1a[:], in_=m_view[1][:, :, 0 : 2 * QT])
+        load_v(1, 0)
+        nc.sync.dma_start(out=m1b[:], in_=m_view[1][:, :, 2 * QT : NQ])
+        load_v(1, 2)
+
+        def mask_cols(c, q0, q1):
+            if q0 < 2 * QT:
+                return (m0a, m1a)[c][:, :, q0:q1]
+            return (m0b, m1b)[c][:, :, q0 - 2 * QT : q1 - 2 * QT]
+
+        def quantize(codes, scales, values):
+            nc.vector.quantize_mx(out=codes.bitcast(FP8X4), scales=scales, in_=values)
+
+        def cast_k(copy, c, s0, s1):
+            copy(
+                out=k_bf[c][:, :, s0:s1, :].rearrange("p r s j -> p s r j"),
+                in_=k_raw[c][:, :, PACK * s0 : PACK * s1].rearrange("p j (s r) -> p s r j", r=PACK),
+            )
+
+        def quant_k(c):
+            quantize(k_codes[c][:], k_scales[c][:], k_bf[c][:].rearrange("p r s j -> p (r s j)"))
+
+        def cast_q(i):
+            src = q_raw[i][:]
+            nc.scalar.copy(
+                out=q_bf[i][:].rearrange("p (c x) j -> p c j x", x=4),
+                in_=src.rearrange("p j (c x) -> p c j x", x=4),
+            )
+
+        def cast_q_gpsimd(i):
+            nc.gpsimd.tensor_scalar(
+                out=q_bf[i][:], in0=q_raw[i][:].rearrange("p j n -> p n j"), scalar1=1.0, scalar2=0.0, op0=ALU.mult, op1=ALU.add
+            )
+
+        def quant_q(i):
+            quantize(q_codes[i][:], q_scales[i][:], q_bf[i][:].rearrange("p n j -> p (n j)"))
+
+        def scale_mask_vector(c, q0, q1):
+            cols = mask_cols(c, q0, q1)
+            for j in range(PACK):
+                nc.vector.tensor_scalar(
+                    out=cols[:, j, :], in0=cols[:, j, :], scalar1=t_root[:, c, j : j + 1], scalar2=None, op0=ALU.mult
+                )
+
+        def scale_mask_scalar(c, q0, q1):
+            cols = mask_cols(c, q0, q1)
+            for j in range(PACK):
+                nc.scalar.activation(out=cols[:, j, :], in_=cols[:, j, :], func=ACT.Copy, scale=t_root[:, c, j : j + 1])
+
+        def cast_v(c, h0, h1):
+            nc.gpsimd.tensor_tensor(
+                out=v_bf[:, 0 : h1 - h0],
+                in0=v_raw[c, h0][:].rearrange("p h j e -> p h e j"),
+                in1=t_sign[:, c, :].unsqueeze(1).unsqueeze(1).to_broadcast([P, h1 - h0, D, PACK]),
+                op=ALU.mult,
+            )
+
+        def quant_v(c, h0, h1):
+            quantize(
+                v_codes[c][:, h0 * D : h1 * D],
+                v_scales[c][:, h0 * D : h1 * D],
+                v_bf[:, 0 : h1 - h0].rearrange("p h e j -> p (h e j)"),
+            )
+
+        def scores(n, h):
+            c, qt = divmod(n, QTILES)
+            i = [x for x, (a, b) in enumerate(q_parts) if a <= qt < b][0]
+            q0 = (qt - q_parts[i][0]) * QT
+            rows = slice(ROWS * h, ROWS * (h + 1))
+            for r in range(PACK):
+                nc.tensor.matmul_mx(
+                    out=score[h][:, r, :],
+                    lhsT=k_codes[c][rows, r * P : (r + 1) * P].bitcast(FP8X4),
+                    lhsT_scale=k_scales[c][rows, r * P : (r + 1) * P],
+                    rhs=q_codes[i][rows, q0 : q0 + QT].bitcast(FP8X4),
+                    rhs_scale=q_scales[i][rows, q0 : q0 + QT],
+                    start=True,
+                    stop=True,
+                )
+
+        def gate(n, h):
+            c, qt = divmod(n, QTILES)
+            a = holder(groups(n), h)
+            nc.vector.scalar_tensor_tensor(
+                out=roots[n, a][:, :, (h - a) * QT : (h - a + 1) * QT],
+                in0=score[h][:],
+                scalar=0.0,
+                in1=mask_cols(c, qt * QT, (qt + 1) * QT),
+                op0=ALU.max,
+                op1=ALU.mult,
+            )
+            if n + 1 < STEPS and (n, h) not in late_scores:
+                scores(n + 1, h)
+
+        def square(n, g):
+            a, b = groups(n)[g]
+            ua = holder(units(n), a)
+            nc.scalar.activation(
+                out=w_bf[n, ua][:, (a - ua) * QT : (b - ua) * QT, :].rearrange("p (c x) r -> p c r x", x=4),
+                in_=roots[n, a][:].rearrange("p r (c x) -> p c r x", x=4),
+                func=ACT.Square,
+            )
+
+        def quant_w(n, g=0):
+            a = units(n)[g][0]
+            quantize(w_codes[n, a][:], w_scales[n, a][:], w_bf[n, a][:].rearrange("p n r -> p (n r)"))
+
+        def y_tile(qt, h0):
+            return ybank[0] if (qt == QTILES - 1 and h0 == 2) else (ybank[1] if (qt == QTILES - 1 and h0 == 3) else ybank[qt])
+
+        def values(qt, h0, h1):
+            for h in range(h0, h1):
+                bank = y_tile(qt, h)
+                for c in range(PASSES):
+                    n = c * QTILES + qt
+                    a = holder(units(n), h)
+                    cols = slice((h - a) * QT, (h - a + 1) * QT)
+                    nc.tensor.matmul_mx(
+                        out=bank[:, h, :],
+                        lhsT=w_codes[n, a][:, cols].bitcast(FP8X4),
+                        lhsT_scale=w_scales[n, a][:, cols],
+                        rhs=v_codes[c][:, h * D : (h + 1) * D].bitcast(FP8X4),
+                        rhs_scale=v_scales[c][:, h * D : (h + 1) * D],
+                        start=(c == 0),
+                        stop=(c == PASSES - 1),
+                    )
+
+        den = {}
+        inv = {}
+
+        def denominators(qt, h0, h1):
+            den[qt, h0] = tile("den%d_%d" % (qt, h0), [P, h1 - h0], F32)
+            nc.scalar.activation(out=den[qt, h0][:], in_=y_tile(qt, h0)[:, h0:h1, D - 1], func=ACT.Copy, bias=1.0)
+
+        def invert(qt, h0, h1):
+            inv[qt, h0] = tile("inv%d_%d" % (qt, h0), [P, h1 - h0], F32)
+            nc.vector.reciprocal(out=inv[qt, h0][:], in_=den[qt, h0][:])
+
+        def finish(qt, h0, h1):
+            res = tile("res%d_%d" % (qt, h0), [P, h1 - h0, D], F32)
+            for h in range(h0, h1):
+                nc.scalar.activation(
+                    out=res[:, h - h0, :], in_=y_tile(qt, h0)[:, h, :], func=ACT.Copy, scale=inv[qt, h0][:, h - h0 : h - h0 + 1]
+                )
+            nc.sync.dma_start(out=out[h0:h1, qt * QT : (qt + 1) * QT, :].rearrange("h q e -> q h e"), in_=res[:])
+
+        def denominators_vector(qt, h0, h1):
+            den[qt, h0] = tile("den%d_%d" % (qt, h0), [P, h1 - h0], F32)
+            nc.vector.tensor_scalar(out=den[qt, h0][:], in0=y_tile(qt, h0)[:, h0:h1, D - 1], scalar1=1.0, scalar2=None, op0=ALU.add)
+
+        def finish_vector(qt, h0, h1):
+            res = tile("res%d_%d" % (qt, h0), [P, h1 - h0, D], F32)
+            nc.vector.tensor_tensor(
+                out=res[:],
+                in0=y_tile(qt, h0)[:, h0:h1, :],
+                in1=inv[qt, h0][:].unsqueeze(2).to_broadcast([P, h1 - h0, D]),
+                op=ALU.mult,
+            )
+            nc.sync.dma_start(out=out[h0:h1, qt * QT : (qt + 1) * QT, :].rearrange("h q e -> q h e"), in_=res[:])
+
+        nc.vector.scalar_tensor_tensor(out=t_abs[:], in0=t_sb[:], scalar=-1.0, in1=t_sb[:], op0=ALU.mult, op1=ALU.max)
+        nc.vector.tensor_scalar(out=t_pos[:], in0=t_sb[:], scalar1=0.0, scalar2=2.0, op0=ALU.is_ge, op1=ALU.mult)
+        nc.scalar.activation(out=guess[:], in_=t_abs[:], func=ACT.Sqrt)
+        nc.vector.tensor_scalar(out=t_sign[:], in0=t_pos[:], scalar1=-1.0, scalar2=None, op0=ALU.add)
+        nc.vector.reciprocal(out=inv_guess[:], in_=guess[:])
+        nc.vector.scalar_tensor_tensor(out=half_quot[:], in0=t_abs[:], scalar=0.5, in1=inv_guess[:], op0=ALU.mult, op1=ALU.mult)
+        nc.vector.scalar_tensor_tensor(out=t_root[:], in0=guess[:], scalar=0.5, in1=half_quot[:], op0=ALU.mult, op1=ALU.add)
+
+        late_scores = {(0, 0), (0, 1), (1, 0), (1, 1), (1, 2), (3, 0), (3, 1), (3, 2)}
+        cast_k(nc.vector.tensor_copy, 0, 0, K_SPLIT)
+        cast_k(nc.scalar.copy, 0, K_SPLIT, P)
+        cast_q(0)
+        quant_k(0)
+        quant_q(0)
+        for h in range(H):
+            scores(0, h)
+        scale_mask_vector(0, 0, QT)
+        scale_mask_scalar(0, QT, 2 * QT)
+        cast_q(1)
+        cast_q_gpsimd(2)
+        gate(0, 0)
+        gate(0, 1)
+        quant_q(1)
+        scores(1, 0)
+        scores(1, 1)
+        square(0, 0)
+        gate(0, 2)
+        gate(0, 3)
+        square(0, 1)
+        scale_mask_scalar(0, 2 * QT, NQ)
+        gate(1, 0)
+        gate(1, 1)
+        gate(1, 2)
+        quant_q(2)
+        quant_w(0)
+        for h in range(3):
+            scores(2, h)
+        cast_v(0, 0, 2)
+        square(1, 0)
+        gate(1, 3)
+        square(1, 1)
+        gate(2, 0)
+        gate(2, 1)
+        gate(2, 2)
+        square(2, 0)
+        quant_w(1)
+        quant_v(0, 0, 2)
+        cast_v(0, 2, 4)
+        gate(2, 3)
+        cast_k(nc.scalar.copy, 1, 0, P)
+        scale_mask_scalar(1, 0, 2 * QT)
+        square(2, 1)
+        gate(3, 0)
+        gate(3, 1)
+        gate(3, 2)
+        quant_k(1)
+        for h in range(3):
+            scores(4, h)
+        quant_v(0, 2, 4)
+        cast_v(1, 0, 2)
+        gate(3, 3)
+        square(3, 0)
+        square(3, 1)
+        gate(4, 0)
+        gate(4, 1)
+        gate(4, 2)
+        quant_w(2)
+        quant_w(3)
+        quant_v(1, 0, 2)
+        cast_v(1, 2, 4)
+        gate(4, 3)
+        square(4, 0)
+        scale_mask_scalar(1, 2 * QT, NQ)
+        square(4, 1)
+        gate(5, 0)
+        gate(5, 1)
+        square(5, 0)
+        gate(5, 2)
+        quant_w(4)
+        values(0, 0, 2)
+        quant_v(1, 2, 4)
+        gate(5, 3)
+        values(0, 2, 4)
+        square(5, 1)
+        gate(6, 0)
+        gate(6, 1)
+        denominators_vector(0, 0, H)
+        square(6, 0)
+        gate(6, 2)
+        invert(0, 0, H)
+        quant_w(5)
+        values(1, 0, 2)
+        finish(0, 0, H)
+        gate(6, 3)
+        values(1, 2, 4)
+        square(6, 1)
+        gate(7, 0)
+        square(7, 0)
+        gate(7, 1)
+        denominators_vector(1, 0, H)
+        square(7, 1)
+        gate(7, 2)
+        invert(1, 0, H)
+        quant_w(6)
+        values(2, 0, H)
+        finish(1, 0, H)
+        square(7, 2)
+        gate(7, 3)
+        square(7, 3)
+        quant_w(7, 0)
+        values(3, 0, 2)
+        denominators_vector(2, 0, H)
+        quant_w(7, 1)
+        values(3, 2, 3)
+        invert(2, 0, H)
+        quant_w(7, 2)
+        values(3, 3, 4)
+        finish(2, 0, H)
+        denominators_vector(3, 0, 2)
+        denominators_vector(3, 2, 3)
+        invert(3, 0, 2)
+        invert(3, 2, 3)
+        denominators_vector(3, 3, 4)
+        finish_vector(3, 0, 2)
+        invert(3, 3, 4)
+        finish_vector(3, 2, 3)
+        finish_vector(3, 3, 4)

@@ -49,7 +49,8 @@ def tile_rows_a_relu2_mask_kernel(tc, qT, kT, t, v, mask, out):
         k_scales = [tile("k_scales%d" % c, [P, PASS], U8) for c in range(PASSES)]
         q_parts = [(0, 1), (1, 2), (2, 4)]
         q_raw = [tile("q_raw%d" % i, [P, PACK, (b - a) * QT], F32) for i, (a, b) in enumerate(q_parts)]
-        q_bf = [tile("q_bf%d" % i, [P, (b - a) * QT, PACK], BF16) for i, (a, b) in enumerate(q_parts)]
+        stage = tile("stage", [P, 2 * QT, PACK], BF16)
+        q_bf = [tile("q_bf0", [P, QT, PACK], BF16), stage[:, 0:QT, :], stage]
         q_codes = [tile("q_codes%d" % i, [P, (b - a) * QT], U32) for i, (a, b) in enumerate(q_parts)]
         q_scales = [tile("q_scales%d" % i, [P, (b - a) * QT], U8) for i, (a, b) in enumerate(q_parts)]
         m0a = tile("m0a", [P, PACK, 2 * QT], F32)
@@ -57,7 +58,6 @@ def tile_rows_a_relu2_mask_kernel(tc, qT, kT, t, v, mask, out):
         m1a = tile("m1a", [P, PACK, 2 * QT], F32)
         m1b = tile("m1b", [P, PACK, 2 * QT], F32)
         v_raw = {(c, h0): tile("v_raw%d_%d" % (c, h0), [P, 2, PACK, D], F32) for c in range(PASSES) for h0 in (0, 2)}
-        v_bf = tile("v_bf", [P, 2, D, PACK], BF16)
         v_codes = [tile("v_codes%d" % c, [P, H * D], U32) for c in range(PASSES)]
         v_scales = [tile("v_scales%d" % c, [P, H * D], U8) for c in range(PASSES)]
 
@@ -154,7 +154,7 @@ def tile_rows_a_relu2_mask_kernel(tc, qT, kT, t, v, mask, out):
 
         def cast_v(c, h0, h1):
             nc.gpsimd.tensor_tensor(
-                out=v_bf[:, 0 : h1 - h0],
+                out=stage[:].rearrange("p (h e) j -> p h e j", h=2),
                 in0=v_raw[c, h0][:].rearrange("p h j e -> p h e j"),
                 in1=t_sign[:, c, :].unsqueeze(1).unsqueeze(1).to_broadcast([P, h1 - h0, D, PACK]),
                 op=ALU.mult,
@@ -164,15 +164,15 @@ def tile_rows_a_relu2_mask_kernel(tc, qT, kT, t, v, mask, out):
             quantize(
                 v_codes[c][:, h0 * D : h1 * D],
                 v_scales[c][:, h0 * D : h1 * D],
-                v_bf[:, 0 : h1 - h0].rearrange("p h e j -> p (h e j)"),
+                stage[:].rearrange("p n j -> p (n j)"),
             )
 
-        def scores(n, h):
+        def score_pass(n, h, r):
             c, qt = divmod(n, QTILES)
             i = [x for x, (a, b) in enumerate(q_parts) if a <= qt < b][0]
             q0 = (qt - q_parts[i][0]) * QT
             rows = slice(ROWS * h, ROWS * (h + 1))
-            for r in range(PACK):
+            if True:
                 nc.tensor.matmul_mx(
                     out=score[h][:, r, :],
                     lhsT=k_codes[c][rows, r * P : (r + 1) * P].bitcast(FP8X4),
@@ -182,6 +182,17 @@ def tile_rows_a_relu2_mask_kernel(tc, qT, kT, t, v, mask, out):
                     start=True,
                     stop=True,
                 )
+
+        pending = []
+        ready = [0]
+
+        def pump(count):
+            for turn in range(count):
+                for item in pending:
+                    if item[2] and item[0] <= ready[0]:
+                        score_pass(item[0], item[1], item[2].pop(0))
+            for item in [x for x in pending if not x[2]]:
+                pending.remove(item)
 
         def gate(n, h):
             c, qt = divmod(n, QTILES)
@@ -194,8 +205,9 @@ def tile_rows_a_relu2_mask_kernel(tc, qT, kT, t, v, mask, out):
                 op0=ALU.max,
                 op1=ALU.mult,
             )
-            if n + 1 < STEPS and (n, h) not in late_scores:
-                scores(n + 1, h)
+            if n + 1 < STEPS:
+                pending.append((n + 1, h, list(range(PACK))))
+            pump(2)
 
         def square(n, g):
             a, b = groups(n)[g]
@@ -271,23 +283,22 @@ def tile_rows_a_relu2_mask_kernel(tc, qT, kT, t, v, mask, out):
         nc.vector.scalar_tensor_tensor(out=half_quot[:], in0=t_abs[:], scalar=0.5, in1=inv_guess[:], op0=ALU.mult, op1=ALU.mult)
         nc.vector.scalar_tensor_tensor(out=t_root[:], in0=guess[:], scalar=0.5, in1=half_quot[:], op0=ALU.mult, op1=ALU.add)
 
-        late_scores = {(0, 0), (0, 1), (1, 0), (1, 1), (1, 2), (3, 0), (3, 1), (3, 2)}
         cast_k(nc.vector.tensor_copy, 0, 0, K_SPLIT)
         cast_k(nc.scalar.copy, 0, K_SPLIT, P)
         cast_q(0)
         quant_k(0)
         quant_q(0)
-        for h in range(H):
-            scores(0, h)
+        pending.extend([(0, h, list(range(PACK))) for h in range(H)])
+        pump(PACK)
         scale_mask_vector(0, 0, QT)
         scale_mask_scalar(0, QT, 2 * QT)
         cast_q(1)
-        cast_q_gpsimd(2)
         gate(0, 0)
         gate(0, 1)
         quant_q(1)
-        scores(1, 0)
-        scores(1, 1)
+        cast_q_gpsimd(2)
+        ready[0] = 1
+        pump(PACK)
         square(0, 0)
         gate(0, 2)
         gate(0, 3)
@@ -295,92 +306,91 @@ def tile_rows_a_relu2_mask_kernel(tc, qT, kT, t, v, mask, out):
         scale_mask_scalar(0, 2 * QT, NQ)
         gate(1, 0)
         gate(1, 1)
-        gate(1, 2)
         quant_q(2)
-        quant_w(0)
-        for h in range(3):
-            scores(2, h)
         cast_v(0, 0, 2)
+        ready[0] = 3
+        pump(PACK)
         square(1, 0)
+        gate(1, 2)
         gate(1, 3)
         square(1, 1)
         gate(2, 0)
         gate(2, 1)
-        gate(2, 2)
         square(2, 0)
-        quant_w(1)
+        gate(2, 2)
+        quant_w(0)
         quant_v(0, 0, 2)
         cast_v(0, 2, 4)
-        gate(2, 3)
         cast_k(nc.scalar.copy, 1, 0, P)
-        scale_mask_scalar(1, 0, 2 * QT)
+        gate(2, 3)
         square(2, 1)
         gate(3, 0)
         gate(3, 1)
+        square(3, 0)
         gate(3, 2)
+        gate(3, 3)
         quant_k(1)
-        for h in range(3):
-            scores(4, h)
+        ready[0] = 7
+        pump(PACK)
+        scale_mask_vector(1, 0, 2 * QT)
+        quant_w(1)
         quant_v(0, 2, 4)
         cast_v(1, 0, 2)
-        gate(3, 3)
-        square(3, 0)
         square(3, 1)
         gate(4, 0)
         gate(4, 1)
+        square(4, 0)
         gate(4, 2)
+        gate(4, 3)
+        square(4, 1)
+        scale_mask_scalar(1, 2 * QT, NQ)
+        gate(5, 0)
         quant_w(2)
         quant_w(3)
         quant_v(1, 0, 2)
         cast_v(1, 2, 4)
-        gate(4, 3)
-        square(4, 0)
-        scale_mask_scalar(1, 2 * QT, NQ)
-        square(4, 1)
-        gate(5, 0)
         gate(5, 1)
         square(5, 0)
         gate(5, 2)
-        quant_w(4)
-        values(0, 0, 2)
-        quant_v(1, 2, 4)
         gate(5, 3)
-        values(0, 2, 4)
         square(5, 1)
         gate(6, 0)
         gate(6, 1)
-        denominators_vector(0, 0, H)
         square(6, 0)
-        gate(6, 2)
-        invert(0, 0, H)
+        quant_w(4)
+        quant_v(1, 2, 4)
+        values(0, 0, 4)
         quant_w(5)
+        gate(6, 2)
         values(1, 0, 2)
-        finish(0, 0, H)
         gate(6, 3)
+        denominators_vector(0, 0, H)
         values(1, 2, 4)
         square(6, 1)
         gate(7, 0)
+        invert(0, 0, H)
+        finish(0, 0, H)
         square(7, 0)
         gate(7, 1)
-        denominators_vector(1, 0, H)
         square(7, 1)
-        gate(7, 2)
-        invert(1, 0, H)
         quant_w(6)
         values(2, 0, H)
-        finish(1, 0, H)
+        denominators_vector(1, 0, H)
+        gate(7, 2)
+        invert(1, 0, H)
         square(7, 2)
         gate(7, 3)
         square(7, 3)
+        finish_vector(1, 0, H)
+        denominators_vector(2, 0, H)
         quant_w(7, 0)
         values(3, 0, 2)
-        denominators_vector(2, 0, H)
+        invert(2, 0, H)
         quant_w(7, 1)
         values(3, 2, 3)
-        invert(2, 0, H)
+        finish(2, 0, H)
         quant_w(7, 2)
         values(3, 3, 4)
-        finish(2, 0, H)
         denominators_vector(3, 0, 2)
         denominators_vector(3, 2, 3)
         invert(3, 0, 2)
@@ -388,5 +398,5 @@ def tile_rows_a_relu2_mask_kernel(tc, qT, kT, t, v, mask, out):
         denominators_vector(3, 3, 4)
         finish_vector(3, 0, 2)
         invert(3, 3, 4)
-        finish_vector(3, 2, 3)
+        finish(3, 2, 3)
         finish_vector(3, 3, 4)

@@ -21,7 +21,12 @@ PASSES = N // PASS
 QT = 128
 QTILES = NQ // QT
 STEPS = PASSES * QTILES
+LAST = STEPS - 1
+RUN = 2
 K_SPLIT = 84
+MASK_SPLIT = 3 * QT
+WINDOW = 5
+FIRST_BATCH = 4
 
 
 def tile_rows_a_relu2_mask_kernel(tc, qT, kT, t, v, mask, out):
@@ -34,369 +39,387 @@ def tile_rows_a_relu2_mask_kernel(tc, qT, kT, t, v, mask, out):
         def tile(name, shape, dtype):
             return sb.tile(shape, dtype, name=name, align_bytes=64)
 
-        t_sb = tile("t_sb", [P, PASSES, PACK], F32)
-        t_abs = tile("t_abs", [P, PASSES, PACK], F32)
-        t_pos = tile("t_pos", [P, PASSES, PACK], F32)
-        t_sign = tile("t_sign", [P, PASSES, PACK], F32)
-        guess = tile("guess", [P, PASSES, PACK], F32)
-        inv_guess = tile("inv_guess", [P, PASSES, PACK], F32)
-        half_quot = tile("half_quot", [P, PASSES, PACK], F32)
-        t_root = tile("t_root", [P, PASSES, PACK], F32)
+        def span_of(spans, x):
+            return [span for span in spans if span[0] <= x < span[1]][0]
+
+        t_sb, t_abs, t_step, t_sign, guess, inv_guess, half_quot, t_root = [
+            tile(name, [P, PASSES, PACK], F32)
+            for name in ("t_sb", "t_abs", "t_step", "t_sign", "guess", "inv_guess", "half_quot", "t_root")
+        ]
 
         k_raw = [tile("k_raw%d" % c, [P, PACK, PASS], F32) for c in range(PASSES)]
         k_bf = [tile("k_bf%d" % c, [P, PACK, P, PACK], BF16) for c in range(PASSES)]
         k_codes = [tile("k_codes%d" % c, [P, PASS], U32) for c in range(PASSES)]
         k_scales = [tile("k_scales%d" % c, [P, PASS], U8) for c in range(PASSES)]
-        q_parts = [(0, 1), (1, 2), (2, 4)]
-        q_raw = [tile("q_raw%d" % i, [P, PACK, (b - a) * QT], F32) for i, (a, b) in enumerate(q_parts)]
+
         stage = tile("stage", [P, 2 * QT, PACK], BF16)
-        q_bf = [tile("q_bf0", [P, QT, PACK], BF16), stage[:, 0:QT, :], stage]
-        q_codes = [tile("q_codes%d" % i, [P, (b - a) * QT], U32) for i, (a, b) in enumerate(q_parts)]
-        q_scales = [tile("q_scales%d" % i, [P, (b - a) * QT], U8) for i, (a, b) in enumerate(q_parts)]
-        m0a = tile("m0a", [P, PACK, 2 * QT], F32)
-        m0b = tile("m0b", [P, PACK, 2 * QT], F32)
-        m1a = tile("m1a", [P, PACK, 2 * QT], F32)
-        m1b = tile("m1b", [P, PACK, 2 * QT], F32)
-        v_raw = {(c, h0): tile("v_raw%d_%d" % (c, h0), [P, 2, PACK, D], F32) for c in range(PASSES) for h0 in (0, 2)}
+
+        q_parts = [(0, 1), (1, 2), (2, 4)]
+        q_raw = {a: tile("q_raw%d" % a, [P, PACK, (b - a) * QT], F32) for a, b in q_parts}
+        q_bf = {0: tile("q_bf0", [P, QT, PACK], BF16)[:], 1: stage[:, 0:QT, :], 2: stage[:]}
+        q_codes = {a: tile("q_codes%d" % a, [P, (b - a) * QT], U32) for a, b in q_parts}
+        q_scales = {a: tile("q_scales%d" % a, [P, (b - a) * QT], U8) for a, b in q_parts}
+
+        mask_parts = [[(0, NQ // 2), (NQ // 2, NQ)], [(0, NQ)]]
+        mask_sb = {
+            (c, a): tile("mask%d_%d" % (c, a), [P, PACK, b - a], F32) for c in range(PASSES) for a, b in mask_parts[c]
+        }
+
+        v_parts = [(c, h0) for c in range(PASSES) for h0 in (0, 2)]
+        v_raw = {part: tile("v_raw%d_%d" % part, [P, 2, PACK, D], F32) for part in v_parts}
         v_codes = [tile("v_codes%d" % c, [P, H * D], U32) for c in range(PASSES)]
         v_scales = [tile("v_scales%d" % c, [P, H * D], U8) for c in range(PASSES)]
 
-        score = [ps.tile([P, PACK, QT], F32, name="score%d" % h) for h in range(H)]
-        ybank = [ps.tile([P, H, D], F32, name="ybank%d" % i) for i in range(QTILES)]
+        def square_spans(n):
+            return [(0, 2), (2, 4)] if n < LAST else [(0, 1), (1, 2), (2, 3), (3, 4)]
 
-        def groups(n):
-            return [(0, 2), (2, 4)] if n < STEPS - 1 else [(0, 1), (1, 2), (2, 3), (3, 4)]
+        def quantize_spans(n):
+            return [(0, 4)] if n < LAST else [(0, 2), (2, 3), (3, 4)]
 
-        def units(n):
-            return [(0, 4)] if n < STEPS - 1 else [(0, 2), (2, 3), (3, 4)]
-
-        roots = {}
-        w_bf = {}
-        w_codes = {}
-        w_scales = {}
+        roots, w_bf, w_codes, w_scales = {}, {}, {}, {}
         for n in range(STEPS):
-            for a, b in groups(n):
+            for a, b in square_spans(n):
                 roots[n, a] = tile("roots%d_%d" % (n, a), [P, PACK, (b - a) * QT], F32)
-            for a, b in units(n):
+            for a, b in quantize_spans(n):
                 w_bf[n, a] = tile("w_bf%d_%d" % (n, a), [P, (b - a) * QT, PACK], BF16)
                 w_codes[n, a] = tile("w_codes%d_%d" % (n, a), [P, (b - a) * QT], U32)
                 w_scales[n, a] = tile("w_scales%d_%d" % (n, a), [P, (b - a) * QT], U8)
 
-        def holder(spans, h):
-            return [a for a, b in spans if a <= h < b][0]
+        score = [ps.tile([P, PACK, QT], F32, name="score%d" % h) for h in range(H)]
+        y_banks = [ps.tile([P, H, D], F32, name="ybank%d" % i) for i in range(QTILES)]
+
+        def y_bank(qt, h):
+            return y_banks[h - 2] if qt == QTILES - 1 and h >= 2 else y_banks[qt]
 
         k_view = kT.rearrange("h (p j) n -> (h p) j n", j=PACK)
         q_view = qT.rearrange("h (p j) n -> (h p) j n", j=PACK)
-        m_view = mask.rearrange("(c p j) q -> c p j q", c=PASSES, j=PACK)
-        v_view = v.rearrange("h (c p j) e -> c p h (j e)", c=PASSES, j=PACK)
-        nc.sync.dma_start(out=t_sb[:], in_=t.rearrange("(c p j) o -> p c (j o)", c=PASSES, j=PACK))
-        nc.sync.dma_start(out=k_raw[0][:], in_=k_view[:, :, 0:PASS])
-        nc.sync.dma_start(out=q_raw[0][:], in_=q_view[:, :, 0:QT])
-        nc.sync.dma_start(out=m0a[:], in_=m_view[0][:, :, 0 : 2 * QT])
-        nc.sync.dma_start(out=q_raw[1][:], in_=q_view[:, :, QT : 2 * QT])
+        mask_view = mask.rearrange("(c p r) q -> c p r q", c=PASSES, r=PACK)
+        v_view = v.rearrange("h (c p r) e -> c p h (r e)", c=PASSES, r=PACK)
 
-        def load_v(c, h0):
-            nc.sync.dma_start(out=v_raw[c, h0][:].rearrange("p h j e -> p h (j e)"), in_=v_view[c][:, h0 : h0 + 2, :])
+        def load_k(c):
+            nc.sync.dma_start(out=k_raw[c][:], in_=k_view[:, :, c * PASS : (c + 1) * PASS])
 
-        nc.sync.dma_start(out=q_raw[2][:], in_=q_view[:, :, 2 * QT : NQ])
-        nc.sync.dma_start(out=m0b[:], in_=m_view[0][:, :, 2 * QT : NQ])
-        load_v(0, 0)
-        load_v(0, 2)
-        nc.sync.dma_start(out=k_raw[1][:], in_=k_view[:, :, PASS:N])
-        nc.sync.dma_start(out=m1a[:], in_=m_view[1][:, :, 0 : 2 * QT])
-        load_v(1, 0)
-        nc.sync.dma_start(out=m1b[:], in_=m_view[1][:, :, 2 * QT : NQ])
-        load_v(1, 2)
+        def load_q(part):
+            a, b = q_parts[part]
+            nc.sync.dma_start(out=q_raw[a][:], in_=q_view[:, :, a * QT : b * QT])
 
-        def mask_cols(c, q0, q1):
-            if q0 < 2 * QT:
-                return (m0a, m1a)[c][:, :, q0:q1]
-            return (m0b, m1b)[c][:, :, q0 - 2 * QT : q1 - 2 * QT]
+        def load_mask(c, part):
+            a, b = mask_parts[c][part]
+            nc.sync.dma_start(out=mask_sb[c, a][:], in_=mask_view[c][:, :, a:b])
+
+        def load_v(part):
+            c, h0 = v_parts[part]
+            nc.sync.dma_start(
+                out=v_raw[c, h0][:].rearrange("p h r e -> p h (r e)"), in_=v_view[c][:, h0 : h0 + 2, :]
+            )
+
+        nc.sync.dma_start(out=t_sb[:], in_=t.rearrange("(c p r) o -> p c (r o)", c=PASSES, r=PACK))
+        load_k(0)
+        load_q(0)
+        load_mask(0, 0)
+        load_q(1)
+        load_q(2)
+        load_mask(0, 1)
+        load_v(0)
+        load_k(1)
+        load_v(1)
+        load_mask(1, 0)
+        load_v(2)
+        load_v(3)
 
         def quantize(codes, scales, values):
             nc.vector.quantize_mx(out=codes.bitcast(FP8X4), scales=scales, in_=values)
 
         def cast_k(copy, c, s0, s1):
             copy(
-                out=k_bf[c][:, :, s0:s1, :].rearrange("p r s j -> p s r j"),
-                in_=k_raw[c][:, :, PACK * s0 : PACK * s1].rearrange("p j (s r) -> p s r j", r=PACK),
+                out=k_bf[c][:, :, s0:s1, :].rearrange("p (a b) s j -> p s a j b", b=RUN),
+                in_=k_raw[c][:, :, PACK * s0 : PACK * s1].rearrange("p j (s a b) -> p s a j b", a=PACK // RUN, b=RUN),
             )
 
-        def quant_k(c):
-            quantize(k_codes[c][:], k_scales[c][:], k_bf[c][:].rearrange("p r s j -> p (r s j)"))
+        def quantize_k(c, r0, r1):
+            cols = slice(r0 * P, r1 * P)
+            quantize(k_codes[c][:, cols], k_scales[c][:, cols], k_bf[c][:, r0:r1].rearrange("p r s j -> p (r s j)"))
 
-        def cast_q(i):
-            src = q_raw[i][:]
+        def cast_q_scalar(a):
             nc.scalar.copy(
-                out=q_bf[i][:].rearrange("p (c x) j -> p c j x", x=4),
-                in_=src.rearrange("p j (c x) -> p c j x", x=4),
+                out=q_bf[a].rearrange("p (c x) j -> p c j x", x=RUN),
+                in_=q_raw[a][:].rearrange("p j (c x) -> p c j x", x=RUN),
             )
 
-        def cast_q_gpsimd(i):
+        def cast_q_gpsimd(a):
             nc.gpsimd.tensor_scalar(
-                out=q_bf[i][:], in0=q_raw[i][:].rearrange("p j n -> p n j"), scalar1=1.0, scalar2=0.0, op0=ALU.mult, op1=ALU.add
+                out=q_bf[a],
+                in0=q_raw[a][:].rearrange("p j n -> p n j"),
+                scalar1=1.0,
+                scalar2=0.0,
+                op0=ALU.mult,
+                op1=ALU.add,
             )
 
-        def quant_q(i):
-            quantize(q_codes[i][:], q_scales[i][:], q_bf[i][:].rearrange("p n j -> p (n j)"))
+        def quantize_q(a):
+            quantize(q_codes[a][:], q_scales[a][:], q_bf[a].rearrange("p n j -> p (n j)"))
+
+        def cast_v(part):
+            c, h0 = v_parts[part]
+            nc.gpsimd.tensor_tensor(
+                out=stage[:].rearrange("p (h e) r -> p h e r", h=2),
+                in0=v_raw[c, h0][:].rearrange("p h r e -> p h e r"),
+                in1=t_sign[:, c, :].unsqueeze(1).unsqueeze(1).to_broadcast([P, 2, D, PACK]),
+                op=ALU.mult,
+            )
+
+        def quantize_v(part):
+            c, h0 = v_parts[part]
+            cols = slice(h0 * D, (h0 + 2) * D)
+            quantize(v_codes[c][:, cols], v_scales[c][:, cols], stage[:].rearrange("p n r -> p (n r)"))
+
+        def mask_cols(c, q0, q1):
+            a = span_of(mask_parts[c], q0)[0]
+            return mask_sb[c, a][:, :, q0 - a : q1 - a]
 
         def scale_mask_vector(c, q0, q1):
             cols = mask_cols(c, q0, q1)
-            for j in range(PACK):
+            for r in range(PACK):
                 nc.vector.tensor_scalar(
-                    out=cols[:, j, :], in0=cols[:, j, :], scalar1=t_root[:, c, j : j + 1], scalar2=None, op0=ALU.mult
+                    out=cols[:, r, :], in0=cols[:, r, :], scalar1=t_root[:, c, r : r + 1], scalar2=None, op0=ALU.mult
                 )
 
         def scale_mask_scalar(c, q0, q1):
             cols = mask_cols(c, q0, q1)
-            for j in range(PACK):
-                nc.scalar.activation(out=cols[:, j, :], in_=cols[:, j, :], func=ACT.Copy, scale=t_root[:, c, j : j + 1])
+            for r in range(PACK):
+                nc.scalar.activation(out=cols[:, r, :], in_=cols[:, r, :], func=ACT.Copy, scale=t_root[:, c, r : r + 1])
 
-        def cast_v(c, h0, h1):
-            nc.gpsimd.tensor_tensor(
-                out=stage[:].rearrange("p (h e) j -> p h e j", h=2),
-                in0=v_raw[c, h0][:].rearrange("p h j e -> p h e j"),
-                in1=t_sign[:, c, :].unsqueeze(1).unsqueeze(1).to_broadcast([P, h1 - h0, D, PACK]),
-                op=ALU.mult,
-            )
-
-        def quant_v(c, h0, h1):
-            quantize(
-                v_codes[c][:, h0 * D : h1 * D],
-                v_scales[c][:, h0 * D : h1 * D],
-                stage[:].rearrange("p n j -> p (n j)"),
-            )
-
-        def score_pass(n, h, r):
+        def score_matmul(n, h, r):
             c, qt = divmod(n, QTILES)
-            i = [x for x, (a, b) in enumerate(q_parts) if a <= qt < b][0]
-            q0 = (qt - q_parts[i][0]) * QT
+            a = span_of(q_parts, qt)[0]
             rows = slice(ROWS * h, ROWS * (h + 1))
-            if True:
-                nc.tensor.matmul_mx(
-                    out=score[h][:, r, :],
-                    lhsT=k_codes[c][rows, r * P : (r + 1) * P].bitcast(FP8X4),
-                    lhsT_scale=k_scales[c][rows, r * P : (r + 1) * P],
-                    rhs=q_codes[i][rows, q0 : q0 + QT].bitcast(FP8X4),
-                    rhs_scale=q_scales[i][rows, q0 : q0 + QT],
-                    start=True,
-                    stop=True,
-                )
+            tokens = slice(r * P, (r + 1) * P)
+            queries = slice((qt - a) * QT, (qt - a + 1) * QT)
+            nc.tensor.matmul_mx(
+                out=score[h][:, r, :],
+                lhsT=k_codes[c][rows, tokens].bitcast(FP8X4),
+                lhsT_scale=k_scales[c][rows, tokens],
+                rhs=q_codes[a][rows, queries].bitcast(FP8X4),
+                rhs_scale=q_scales[a][rows, queries],
+                start=True,
+                stop=True,
+            )
 
-        pending = []
-        ready = [0]
+        to_fill = []
+        quantized_steps = [0]
 
-        def pump(count):
-            for turn in range(count):
-                for item in pending:
-                    if item[2] and item[0] <= ready[0]:
-                        score_pass(item[0], item[1], item[2].pop(0))
-            for item in [x for x in pending if not x[2]]:
-                pending.remove(item)
+        def fill_banks(turns):
+            for turn in range(turns):
+                for n, h, places in to_fill:
+                    if places and n in quantized_steps:
+                        score_matmul(n, h, places.pop(0))
+            for item in [x for x in to_fill if not x[2]]:
+                to_fill.remove(item)
 
-        def gate(n, h):
+        def gate_columns(n, h, q0, q1):
             c, qt = divmod(n, QTILES)
-            a = holder(groups(n), h)
+            a = span_of(square_spans(n), h)[0]
             nc.vector.scalar_tensor_tensor(
-                out=roots[n, a][:, :, (h - a) * QT : (h - a + 1) * QT],
-                in0=score[h][:],
+                out=roots[n, a][:, :, (h - a) * QT + q0 : (h - a) * QT + q1],
+                in0=score[h][:, :, q0:q1],
                 scalar=0.0,
-                in1=mask_cols(c, qt * QT, (qt + 1) * QT),
+                in1=mask_cols(c, qt * QT + q0, qt * QT + q1),
                 op0=ALU.max,
                 op1=ALU.mult,
             )
-            if n + 1 < STEPS:
-                pending.append((n + 1, h, list(range(PACK))))
-            pump(2)
 
-        def square(n, g):
-            a, b = groups(n)[g]
-            ua = holder(units(n), a)
+        def gate(n, h):
+            gate_columns(n, h, 0, QT)
+            if n < LAST:
+                to_fill.append((n + 1, h, list(range(PACK))))
+            fill_banks(PACK // 2)
+
+        def square_columns(n, a, x0, x1):
+            first = (a - span_of(quantize_spans(n), a)[0]) * QT
             nc.scalar.activation(
-                out=w_bf[n, ua][:, (a - ua) * QT : (b - ua) * QT, :].rearrange("p (c x) r -> p c r x", x=4),
-                in_=roots[n, a][:].rearrange("p r (c x) -> p c r x", x=4),
+                out=w_bf[n, span_of(quantize_spans(n), a)[0]][:, first + x0 : first + x1, :].rearrange(
+                    "p (c x) r -> p c r x", x=RUN
+                ),
+                in_=roots[n, a][:, :, x0:x1].rearrange("p r (c x) -> p c r x", x=RUN),
                 func=ACT.Square,
             )
 
-        def quant_w(n, g=0):
-            a = units(n)[g][0]
+        def square(n, h):
+            a, b = span_of(square_spans(n), h)
+            square_columns(n, a, 0, (b - a) * QT)
+
+        def quantize_w(n, h=0):
+            a = span_of(quantize_spans(n), h)[0]
             quantize(w_codes[n, a][:], w_scales[n, a][:], w_bf[n, a][:].rearrange("p n r -> p (n r)"))
 
-        def y_tile(qt, h0):
-            return ybank[0] if (qt == QTILES - 1 and h0 == 2) else (ybank[1] if (qt == QTILES - 1 and h0 == 3) else ybank[qt])
+        def y_matmul(qt, h, c):
+            n = c * QTILES + qt
+            a = span_of(quantize_spans(n), h)[0]
+            queries = slice((h - a) * QT, (h - a + 1) * QT)
+            nc.tensor.matmul_mx(
+                out=y_bank(qt, h)[:, h, :],
+                lhsT=w_codes[n, a][:, queries].bitcast(FP8X4),
+                lhsT_scale=w_scales[n, a][:, queries],
+                rhs=v_codes[c][:, h * D : (h + 1) * D].bitcast(FP8X4),
+                rhs_scale=v_scales[c][:, h * D : (h + 1) * D],
+                start=(c == 0),
+                stop=(c == PASSES - 1),
+            )
 
-        def values(qt, h0, h1):
+        def y_product(qt, h0, h1):
             for h in range(h0, h1):
-                bank = y_tile(qt, h)
                 for c in range(PASSES):
-                    n = c * QTILES + qt
-                    a = holder(units(n), h)
-                    cols = slice((h - a) * QT, (h - a + 1) * QT)
-                    nc.tensor.matmul_mx(
-                        out=bank[:, h, :],
-                        lhsT=w_codes[n, a][:, cols].bitcast(FP8X4),
-                        lhsT_scale=w_scales[n, a][:, cols],
-                        rhs=v_codes[c][:, h * D : (h + 1) * D].bitcast(FP8X4),
-                        rhs_scale=v_scales[c][:, h * D : (h + 1) * D],
-                        start=(c == 0),
-                        stop=(c == PASSES - 1),
-                    )
+                    y_matmul(qt, h, c)
 
-        den = {}
-        inv = {}
+        den, inv = {}, {}
 
         def denominators(qt, h0, h1):
             den[qt, h0] = tile("den%d_%d" % (qt, h0), [P, h1 - h0], F32)
-            nc.scalar.activation(out=den[qt, h0][:], in_=y_tile(qt, h0)[:, h0:h1, D - 1], func=ACT.Copy, bias=1.0)
+            nc.vector.tensor_scalar(
+                out=den[qt, h0][:], in0=y_bank(qt, h0)[:, h0:h1, D - 1], scalar1=1.0, scalar2=None, op0=ALU.add
+            )
 
         def invert(qt, h0, h1):
             inv[qt, h0] = tile("inv%d_%d" % (qt, h0), [P, h1 - h0], F32)
             nc.vector.reciprocal(out=inv[qt, h0][:], in_=den[qt, h0][:])
 
-        def finish(qt, h0, h1):
+        def store(qt, h0, h1, res):
+            nc.sync.dma_start(out=out[h0:h1, qt * QT : (qt + 1) * QT, :].rearrange("h q e -> q h e"), in_=res[:])
+
+        def divide_scalar(qt, h0, h1):
             res = tile("res%d_%d" % (qt, h0), [P, h1 - h0, D], F32)
             for h in range(h0, h1):
                 nc.scalar.activation(
-                    out=res[:, h - h0, :], in_=y_tile(qt, h0)[:, h, :], func=ACT.Copy, scale=inv[qt, h0][:, h - h0 : h - h0 + 1]
+                    out=res[:, h - h0, :],
+                    in_=y_bank(qt, h)[:, h, :],
+                    func=ACT.Copy,
+                    scale=inv[qt, h0][:, h - h0 : h - h0 + 1],
                 )
-            nc.sync.dma_start(out=out[h0:h1, qt * QT : (qt + 1) * QT, :].rearrange("h q e -> q h e"), in_=res[:])
+            store(qt, h0, h1, res)
 
-        def denominators_vector(qt, h0, h1):
-            den[qt, h0] = tile("den%d_%d" % (qt, h0), [P, h1 - h0], F32)
-            nc.vector.tensor_scalar(out=den[qt, h0][:], in0=y_tile(qt, h0)[:, h0:h1, D - 1], scalar1=1.0, scalar2=None, op0=ALU.add)
-
-        def finish_vector(qt, h0, h1):
+        def divide_vector(qt, h0, h1):
             res = tile("res%d_%d" % (qt, h0), [P, h1 - h0, D], F32)
             nc.vector.tensor_tensor(
                 out=res[:],
-                in0=y_tile(qt, h0)[:, h0:h1, :],
+                in0=y_bank(qt, h0)[:, h0:h1, :],
                 in1=inv[qt, h0][:].unsqueeze(2).to_broadcast([P, h1 - h0, D]),
                 op=ALU.mult,
             )
-            nc.sync.dma_start(out=out[h0:h1, qt * QT : (qt + 1) * QT, :].rearrange("h q e -> q h e"), in_=res[:])
+            store(qt, h0, h1, res)
 
         nc.vector.scalar_tensor_tensor(out=t_abs[:], in0=t_sb[:], scalar=-1.0, in1=t_sb[:], op0=ALU.mult, op1=ALU.max)
-        nc.vector.tensor_scalar(out=t_pos[:], in0=t_sb[:], scalar1=0.0, scalar2=2.0, op0=ALU.is_ge, op1=ALU.mult)
+        nc.vector.tensor_scalar(out=t_step[:], in0=t_sb[:], scalar1=0.0, scalar2=2.0, op0=ALU.is_ge, op1=ALU.mult)
         nc.scalar.activation(out=guess[:], in_=t_abs[:], func=ACT.Sqrt)
-        nc.vector.tensor_scalar(out=t_sign[:], in0=t_pos[:], scalar1=-1.0, scalar2=None, op0=ALU.add)
+        nc.vector.tensor_scalar(out=t_sign[:], in0=t_step[:], scalar1=-1.0, scalar2=None, op0=ALU.add)
         nc.vector.reciprocal(out=inv_guess[:], in_=guess[:])
-        nc.vector.scalar_tensor_tensor(out=half_quot[:], in0=t_abs[:], scalar=0.5, in1=inv_guess[:], op0=ALU.mult, op1=ALU.mult)
-        nc.vector.scalar_tensor_tensor(out=t_root[:], in0=guess[:], scalar=0.5, in1=half_quot[:], op0=ALU.mult, op1=ALU.add)
+        nc.vector.scalar_tensor_tensor(
+            out=half_quot[:], in0=t_abs[:], scalar=0.5, in1=inv_guess[:], op0=ALU.mult, op1=ALU.mult
+        )
+        nc.vector.scalar_tensor_tensor(
+            out=t_root[:], in0=guess[:], scalar=0.5, in1=half_quot[:], op0=ALU.mult, op1=ALU.add
+        )
 
         cast_k(nc.vector.tensor_copy, 0, 0, K_SPLIT)
         cast_k(nc.scalar.copy, 0, K_SPLIT, P)
-        cast_q(0)
-        quant_k(0)
-        quant_q(0)
-        pending.extend([(0, h, list(range(PACK))) for h in range(H)])
-        pump(PACK)
+        cast_q_scalar(0)
+        quantize_k(0, 0, PACK)
+        quantize_q(0)
+        to_fill.extend([(0, h, list(range(PACK))) for h in range(H)])
+        fill_banks(PACK)
         scale_mask_vector(0, 0, QT)
         scale_mask_scalar(0, QT, 2 * QT)
-        cast_q(1)
-        gate(0, 0)
-        gate(0, 1)
-        quant_q(1)
-        cast_q_gpsimd(2)
-        ready[0] = 1
-        pump(PACK)
-        square(0, 0)
-        gate(0, 2)
-        gate(0, 3)
-        square(0, 1)
-        scale_mask_scalar(0, 2 * QT, NQ)
-        gate(1, 0)
-        gate(1, 1)
-        quant_q(2)
-        cast_v(0, 0, 2)
-        ready[0] = 3
-        pump(PACK)
-        square(1, 0)
-        gate(1, 2)
-        gate(1, 3)
-        square(1, 1)
-        gate(2, 0)
-        gate(2, 1)
-        square(2, 0)
-        gate(2, 2)
-        quant_w(0)
-        quant_v(0, 0, 2)
-        cast_v(0, 2, 4)
-        cast_k(nc.scalar.copy, 1, 0, P)
-        gate(2, 3)
-        square(2, 1)
-        gate(3, 0)
-        gate(3, 1)
-        square(3, 0)
-        gate(3, 2)
-        gate(3, 3)
-        quant_k(1)
-        ready[0] = 7
-        pump(PACK)
-        scale_mask_vector(1, 0, 2 * QT)
-        quant_w(1)
-        quant_v(0, 2, 4)
-        cast_v(1, 0, 2)
-        square(3, 1)
-        gate(4, 0)
-        gate(4, 1)
-        square(4, 0)
-        gate(4, 2)
-        gate(4, 3)
-        square(4, 1)
-        scale_mask_scalar(1, 2 * QT, NQ)
-        gate(5, 0)
-        quant_w(2)
-        quant_w(3)
-        quant_v(1, 0, 2)
-        cast_v(1, 2, 4)
-        gate(5, 1)
-        square(5, 0)
-        gate(5, 2)
-        gate(5, 3)
-        square(5, 1)
-        gate(6, 0)
+        cast_q_scalar(1)
+
+        def batch(b):
+            if b == 0:
+                quantize_q(2)
+                quantized_steps.extend([2, 3])
+                fill_banks(PACK // 2)
+            if b == 1:
+                quantize_w(0)
+            if b == 2:
+                quantize_k(1, 0, PACK)
+                quantized_steps.extend(range(QTILES, STEPS))
+                fill_banks(PACK)
+                scale_mask_vector(1, 0, MASK_SPLIT)
+            if b == 3:
+                quantize_w(1)
+            if b == 4:
+                quantize_w(QTILES)
+                y_product(0, 0, 2)
+            if b > 0:
+                quantize_v(b - 1)
+            if b < len(v_parts):
+                cast_v(b)
+
+        scalar_extras = {
+            1 * H + 1: lambda: scale_mask_scalar(0, 2 * QT, NQ),
+            1 * H + 3: lambda: cast_k(nc.scalar.copy, 1, 0, P),
+            3 * H + 1: lambda: scale_mask_scalar(1, MASK_SPLIT, NQ),
+        }
+
+        for slot in range(FIRST_BATCH + len(v_parts) * WINDOW + 1):
+            n, h = divmod(slot, H)
+            gate(n, h)
+            if slot == 0:
+                quantize_q(1)
+                cast_q_gpsimd(2)
+                quantized_steps.append(1)
+                fill_banks(PACK // 2)
+            if slot >= FIRST_BATCH and (slot - FIRST_BATCH) % WINDOW == 0:
+                batch((slot - FIRST_BATCH) // WINDOW)
+            if slot in scalar_extras:
+                scalar_extras[slot]()
+            if h % 2 == 1:
+                square(n, h)
+
+        y_product(0, 2, H)
+        quantize_w(2)
         gate(6, 1)
-        square(6, 0)
-        quant_w(4)
-        quant_v(1, 2, 4)
-        values(0, 0, 4)
-        quant_w(5)
-        gate(6, 2)
-        values(1, 0, 2)
-        gate(6, 3)
-        denominators_vector(0, 0, H)
-        values(1, 2, 4)
         square(6, 1)
-        gate(7, 0)
+        quantize_w(5)
+        y_product(1, 0, 2)
+        denominators(0, 0, H)
+        gate(6, 2)
         invert(0, 0, H)
-        finish(0, 0, H)
-        square(7, 0)
-        gate(7, 1)
-        square(7, 1)
-        quant_w(6)
-        values(2, 0, H)
-        denominators_vector(1, 0, H)
-        gate(7, 2)
+        y_product(1, 2, H)
+        divide_scalar(0, 0, H)
+        gate(6, 3)
+        square(6, 3)
+        quantize_w(3)
+        gate(LAST, 0)
+        denominators(1, 0, H)
+        square(LAST, 0)
+        gate(LAST, 1)
         invert(1, 0, H)
-        square(7, 2)
-        gate(7, 3)
-        square(7, 3)
-        finish_vector(1, 0, H)
-        denominators_vector(2, 0, H)
-        quant_w(7, 0)
-        values(3, 0, 2)
+        square(LAST, 1)
+        quantize_w(6)
+        y_product(2, 0, H)
+        y_matmul(3, 2, 0)
+        divide_scalar(1, 0, H)
+        y_matmul(3, 3, 0)
+        gate(LAST, 2)
+        square(LAST, 2)
+        quantize_w(LAST, 0)
+        y_product(3, 0, 2)
+        halves = [(0, QT // 2), (QT // 2, QT)]
+        for q0, q1 in halves:
+            gate_columns(LAST, 3, q0, q1)
+        for q0, q1 in halves:
+            square_columns(LAST, 3, q0, q1)
+        denominators(2, 0, H)
         invert(2, 0, H)
-        quant_w(7, 1)
-        values(3, 2, 3)
-        finish(2, 0, H)
-        quant_w(7, 2)
-        values(3, 3, 4)
-        denominators_vector(3, 0, 2)
-        denominators_vector(3, 2, 3)
+        divide_vector(2, 0, H)
+        quantize_w(LAST, 2)
+        y_matmul(3, 2, 1)
+        denominators(3, 0, 2)
+        quantize_w(LAST, 3)
+        y_matmul(3, 3, 1)
         invert(3, 0, 2)
+        denominators(3, 2, 3)
+        divide_scalar(3, 0, 2)
         invert(3, 2, 3)
-        denominators_vector(3, 3, 4)
-        finish_vector(3, 0, 2)
+        denominators(3, 3, 4)
+        divide_vector(3, 2, 3)
         invert(3, 3, 4)
-        finish(3, 2, 3)
-        finish_vector(3, 3, 4)
+        divide_vector(3, 3, 4)

@@ -24,7 +24,6 @@ STEPS = PASSES * QTILES
 LAST = STEPS - 1
 RUN = 2
 K_SPLIT = 84
-MASK_SPLIT = 3 * QT
 WINDOW = 5
 FIRST_BATCH = 4
 
@@ -140,8 +139,8 @@ def tile_rows_a_relu2_mask_kernel(tc, qT, kT, t, v, mask, out):
             cols = slice(r0 * P, r1 * P)
             quantize(k_codes[c][:, cols], k_scales[c][:, cols], k_bf[c][:, r0:r1].rearrange("p r s j -> p (r s j)"))
 
-        def cast_q_scalar(a):
-            nc.scalar.copy(
+        def cast_q(copy, a):
+            copy(
                 out=q_bf[a].rearrange("p (c x) j -> p c j x", x=RUN),
                 in_=q_raw[a][:].rearrange("p j (c x) -> p c j x", x=RUN),
             )
@@ -321,17 +320,19 @@ def tile_rows_a_relu2_mask_kernel(tc, qT, kT, t, v, mask, out):
 
         cast_k(nc.vector.tensor_copy, 0, 0, K_SPLIT)
         cast_k(nc.scalar.copy, 0, K_SPLIT, P)
-        cast_q_scalar(0)
-        quantize_k(0, 0, PACK)
+        cast_q(nc.vector.tensor_copy, 0)
+        quantize_k(0, 0, PACK // 2)
         quantize_q(0)
+        quantize_k(0, PACK // 2, PACK)
         to_fill.extend([(0, h, list(range(PACK))) for h in range(H)])
         fill_banks(PACK)
         scale_mask_vector(0, 0, QT)
         scale_mask_scalar(0, QT, 2 * QT)
-        cast_q_scalar(1)
+        cast_q(nc.scalar.copy, 1)
 
         def batch(b):
             if b == 0:
+                scale_mask_vector(0, 2 * QT, NQ)
                 quantize_q(2)
                 quantized_steps.extend([2, 3])
                 fill_banks(PACK // 2)
@@ -341,7 +342,7 @@ def tile_rows_a_relu2_mask_kernel(tc, qT, kT, t, v, mask, out):
                 quantize_k(1, 0, PACK)
                 quantized_steps.extend(range(QTILES, STEPS))
                 fill_banks(PACK)
-                scale_mask_vector(1, 0, MASK_SPLIT)
+                scale_mask_vector(1, 0, NQ)
             if b == 3:
                 quantize_w(1)
             if b == 4:
@@ -353,19 +354,17 @@ def tile_rows_a_relu2_mask_kernel(tc, qT, kT, t, v, mask, out):
                 cast_v(b)
 
         scalar_extras = {
-            1 * H + 1: lambda: scale_mask_scalar(0, 2 * QT, NQ),
             1 * H + 3: lambda: cast_k(nc.scalar.copy, 1, 0, P),
-            3 * H + 1: lambda: scale_mask_scalar(1, MASK_SPLIT, NQ),
         }
 
         for slot in range(FIRST_BATCH + len(v_parts) * WINDOW + 1):
             n, h = divmod(slot, H)
             gate(n, h)
-            if slot == 0:
+            if slot == 1:
                 quantize_q(1)
                 cast_q_gpsimd(2)
                 quantized_steps.append(1)
-                fill_banks(PACK // 2)
+                fill_banks(PACK)
             if slot >= FIRST_BATCH and (slot - FIRST_BATCH) % WINDOW == 0:
                 batch((slot - FIRST_BATCH) // WINDOW)
             if slot in scalar_extras:

@@ -118,8 +118,8 @@ def tile_rows_a_relu2_mask_kernel(tc, qT, kT, t, v, mask, out):
         load_mask(0, 0)
         load_q(1)
         load_q(2)
-        load_mask(0, 1)
         load_v(0)
+        load_mask(0, 1)
         load_k(1)
         load_v(1)
         load_mask(1, 0)
@@ -332,7 +332,6 @@ def tile_rows_a_relu2_mask_kernel(tc, qT, kT, t, v, mask, out):
 
         def batch(b):
             if b == 0:
-                scale_mask_vector(0, 2 * QT, NQ)
                 quantize_q(2)
                 quantized_steps.extend([2, 3])
                 fill_banks(PACK // 2)
@@ -354,6 +353,7 @@ def tile_rows_a_relu2_mask_kernel(tc, qT, kT, t, v, mask, out):
                 cast_v(b)
 
         scalar_extras = {
+            1 * H + 1: lambda: scale_mask_scalar(0, 2 * QT, NQ),
             1 * H + 3: lambda: cast_k(nc.scalar.copy, 1, 0, P),
         }
 
@@ -399,14 +399,14 @@ def tile_rows_a_relu2_mask_kernel(tc, qT, kT, t, v, mask, out):
         y_matmul(3, 3, 0)
         gate(LAST, 2)
         square(LAST, 2)
-        quantize_w(LAST, 0)
-        y_product(3, 0, 2)
         halves = [(0, QT // 2), (QT // 2, QT)]
         for q0, q1 in halves:
             gate_columns(LAST, 3, q0, q1)
         for q0, q1 in halves:
             square_columns(LAST, 3, q0, q1)
         denominators(2, 0, H)
+        quantize_w(LAST, 0)
+        y_product(3, 0, 2)
         invert(2, 0, H)
         divide_vector(2, 0, H)
         quantize_w(LAST, 2)

from contextlib import ExitStack

import concourse.mybir as mybir

H, D, NQ, N = 4, 128, 512, 1024
FLOPS = 2 * 2 * H * N * NQ * D

F32 = mybir.dt.float32
BF16 = mybir.dt.bfloat16
U32 = mybir.dt.uint32
U8 = mybir.dt.uint8
FP8X4 = mybir.dt.float8_e4m3fn_x4
ALU = mybir.AluOpType
ACT = mybir.ActivationFunctionType

P = 128
PACK = 4
ROWS = D // PACK
PASS = P * PACK
PASSES = N // PASS
QT = 128
QTILES = NQ // QT
STEPS = PASSES * QTILES
LAST = STEPS - 1
RUN = 2
K_SPLIT = 84
WINDOW = 5
FIRST_BATCH = 4


def tile_rows_a_relu2_mask_kernel(tc, qT, kT, t, v, mask, out):
    nc = tc.nc
    with ExitStack() as ctx:
        sb = ctx.enter_context(tc.tile_pool(name="sb", bufs=1))
        ps = ctx.enter_context(tc.psum_pool(name="ps", bufs=1))
        ctx.enter_context(tc.manual_schedule())

        def tile(name, shape, dtype):
            return sb.tile(shape, dtype, name=name, align_bytes=64)

        def span_of(spans, x):
            return [span for span in spans if span[0] <= x < span[1]][0]

        t_sb, t_abs, t_step, t_sign, guess, inv_guess, half_quot, t_root = [
            tile(name, [P, PASSES, PACK], F32)
            for name in ("t_sb", "t_abs", "t_step", "t_sign", "guess", "inv_guess", "half_quot", "t_root")
        ]

        k_raw = [tile("k_raw%d" % c, [P, PACK, PASS], F32) for c in range(PASSES)]
        k_bf = [tile("k_bf%d" % c, [P, PACK, P, PACK], BF16) for c in range(PASSES)]
        k_codes = [tile("k_codes%d" % c, [P, PASS], U32) for c in range(PASSES)]
        k_scales = [tile("k_scales%d" % c, [P, PASS], U8) for c in range(PASSES)]

        stage = tile("stage", [P, 2 * QT, PACK], BF16)

        q_parts = [(0, 1), (1, 2), (2, 4)]
        q_raw = {a: tile("q_raw%d" % a, [P, PACK, (b - a) * QT], F32) for a, b in q_parts}
        q_bf = {0: tile("q_bf0", [P, QT, PACK], BF16)[:], 1: stage[:, 0:QT, :], 2: stage[:]}
        q_codes = {a: tile("q_codes%d" % a, [P, (b - a) * QT], U32) for a, b in q_parts}
        q_scales = {a: tile("q_scales%d" % a, [P, (b - a) * QT], U8) for a, b in q_parts}

        mask_parts = [[(0, NQ // 2), (NQ // 2, NQ)], [(0, NQ)]]
        mask_sb = {
            (c, a): tile("mask%d_%d" % (c, a), [P, PACK, b - a], F32) for c in range(PASSES) for a, b in mask_parts[c]
        }

        v_parts = [(c, h0) for c in range(PASSES) for h0 in (0, 2)]
        v_raw = {part: tile("v_raw%d_%d" % part, [P, 2, PACK, D], F32) for part in v_parts}
        v_codes = [tile("v_codes%d" % c, [P, H * D], U32) for c in range(PASSES)]
        v_scales = [tile("v_scales%d" % c, [P, H * D], U8) for c in range(PASSES)]

        def square_spans(n):
            return [(0, 2), (2, 4)] if n < LAST else [(0, 1), (1, 2), (2, 3), (3, 4)]

        def quantize_spans(n):
            return [(0, 4)] if n < LAST else [(0, 2), (2, 3), (3, 4)]

        roots, w_bf, w_codes, w_scales = {}, {}, {}, {}
        for n in range(STEPS):
            for a, b in square_spans(n):
                roots[n, a] = tile("roots%d_%d" % (n, a), [P, PACK, (b - a) * QT], F32)
            for a, b in quantize_spans(n):
                w_bf[n, a] = tile("w_bf%d_%d" % (n, a), [P, (b - a) * QT, PACK], BF16)
                w_codes[n, a] = tile("w_codes%d_%d" % (n, a), [P, (b - a) * QT], U32)
                w_scales[n, a] = tile("w_scales%d_%d" % (n, a), [P, (b - a) * QT], U8)

        score = [ps.tile([P, PACK, QT], F32, name="score%d" % h) for h in range(H)]
        y_banks = [ps.tile([P, H, D], F32, name="ybank%d" % i) for i in range(QTILES)]

        def y_bank(qt, h):
            return y_banks[h - 2] if qt == QTILES - 1 and h >= 2 else y_banks[qt]

        k_view = kT.rearrange("h (p j) n -> (h p) j n", j=PACK)
        q_view = qT.rearrange("h (p j) n -> (h p) j n", j=PACK)
        mask_view = mask.rearrange("(c p r) q -> c p r q", c=PASSES, r=PACK)
        v_view = v.rearrange("h (c p r) e -> c p h (r e)", c=PASSES, r=PACK)

        def load_k(c):
            nc.sync.dma_start(out=k_raw[c][:], in_=k_view[:, :, c * PASS : (c + 1) * PASS])

        def load_q(part):
            a, b = q_parts[part]
            nc.sync.dma_start(out=q_raw[a][:], in_=q_view[:, :, a * QT : b * QT])

        def load_mask(c, part):
            a, b = mask_parts[c][part]
            nc.sync.dma_start(out=mask_sb[c, a][:], in_=mask_view[c][:, :, a:b])

        def load_v(part):
            c, h0 = v_parts[part]
            nc.sync.dma_start(
                out=v_raw[c, h0][:].rearrange("p h r e -> p h (r e)"), in_=v_view[c][:, h0 : h0 + 2, :]
            )

        nc.sync.dma_start(out=t_sb[:], in_=t.rearrange("(c p r) o -> p c (r o)", c=PASSES, r=PACK))
        load_k(0)
        load_q(0)
        load_mask(0, 0)
        load_q(1)
        load_q(2)
        load_v(0)
        load_mask(0, 1)
        load_k(1)
        load_v(1)
        load_mask(1, 0)
        load_v(2)
        load_v(3)

        def quantize(codes, scales, values):
            nc.vector.quantize_mx(out=codes.bitcast(FP8X4), scales=scales, in_=values)

        def cast_k(copy, c, s0, s1):
            copy(
                out=k_bf[c][:, :, s0:s1, :].rearrange("p (a b) s j -> p s a j b", b=RUN),
                in_=k_raw[c][:, :, PACK * s0 : PACK * s1].rearrange("p j (s a b) -> p s a j b", a=PACK // RUN, b=RUN),
            )

        def quantize_k(c, r0, r1):
            cols = slice(r0 * P, r1 * P)
            quantize(k_codes[c][:, cols], k_scales[c][:, cols], k_bf[c][:, r0:r1].rearrange("p r s j -> p (r s j)"))

        def cast_q(copy, a):
            copy(
                out=q_bf[a].rearrange("p (c x) j -> p c j x", x=RUN),
                in_=q_raw[a][:].rearrange("p j (c x) -> p c j x", x=RUN),
            )

        def cast_q_gpsimd(a):
            nc.gpsimd.tensor_scalar(
                out=q_bf[a],
                in0=q_raw[a][:].rearrange("p j n -> p n j"),
                scalar1=1.0,
                scalar2=0.0,
                op0=ALU.mult,
                op1=ALU.add,
            )

        def quantize_q(a):
            quantize(q_codes[a][:], q_scales[a][:], q_bf[a].rearrange("p n j -> p (n j)"))

        def cast_v(part):
            c, h0 = v_parts[part]
            nc.gpsimd.tensor_tensor(
                out=stage[:].rearrange("p (h e) r -> p h e r", h=2),
                in0=v_raw[c, h0][:].rearrange("p h r e -> p h e r"),
                in1=t_sign[:, c, :].unsqueeze(1).unsqueeze(1).to_broadcast([P, 2, D, PACK]),
                op=ALU.mult,
            )

        def quantize_v(part):
            c, h0 = v_parts[part]
            cols = slice(h0 * D, (h0 + 2) * D)
            quantize(v_codes[c][:, cols], v_scales[c][:, cols], stage[:].rearrange("p n r -> p (n r)"))

        def mask_cols(c, q0, q1):
            a = span_of(mask_parts[c], q0)[0]
            return mask_sb[c, a][:, :, q0 - a : q1 - a]

        def scale_mask_vector(c, q0, q1):
            cols = mask_cols(c, q0, q1)
            for r in range(PACK):
                nc.vector.tensor_scalar(
                    out=cols[:, r, :], in0=cols[:, r, :], scalar1=t_root[:, c, r : r + 1], scalar2=None, op0=ALU.mult
                )

        def scale_mask_scalar(c, q0, q1):
            cols = mask_cols(c, q0, q1)
            for r in range(PACK):
                nc.scalar.activation(out=cols[:, r, :], in_=cols[:, r, :], func=ACT.Copy, scale=t_root[:, c, r : r + 1])

        def score_matmul(n, h, r):
            c, qt = divmod(n, QTILES)
            a = span_of(q_parts, qt)[0]
            rows = slice(ROWS * h, ROWS * (h + 1))
            tokens = slice(r * P, (r + 1) * P)
            queries = slice((qt - a) * QT, (qt - a + 1) * QT)
            nc.tensor.matmul_mx(
                out=score[h][:, r, :],
                lhsT=k_codes[c][rows, tokens].bitcast(FP8X4),
                lhsT_scale=k_scales[c][rows, tokens],
                rhs=q_codes[a][rows, queries].bitcast(FP8X4),
                rhs_scale=q_scales[a][rows, queries],
                start=True,
                stop=True,
            )

        to_fill = []
        quantized_steps = [0]

        def fill_banks(turns):
            for turn in range(turns):
                for n, h, places in to_fill:
                    if places and n in quantized_steps:
                        score_matmul(n, h, places.pop(0))
            for item in [x for x in to_fill if not x[2]]:
                to_fill.remove(item)

        def gate_columns(n, h, q0, q1):
            c, qt = divmod(n, QTILES)
            a = span_of(square_spans(n), h)[0]
            nc.vector.scalar_tensor_tensor(
                out=roots[n, a][:, :, (h - a) * QT + q0 : (h - a) * QT + q1],
                in0=score[h][:, :, q0:q1],
                scalar=0.0,
                in1=mask_cols(c, qt * QT + q0, qt * QT + q1),
                op0=ALU.max,
                op1=ALU.mult,
            )

        def gate(n, h):
            gate_columns(n, h, 0, QT)
            if n < LAST:
                to_fill.append((n + 1, h, list(range(PACK))))
            fill_banks(PACK // 2)

        def square_columns(n, a, x0, x1):
            first = (a - span_of(quantize_spans(n), a)[0]) * QT
            nc.scalar.activation(
                out=w_bf[n, span_of(quantize_spans(n), a)[0]][:, first + x0 : first + x1, :].rearrange(
                    "p (c x) r -> p c r x", x=RUN
                ),
                in_=roots[n, a][:, :, x0:x1].rearrange("p r (c x) -> p c r x", x=RUN),
                func=ACT.Square,
            )

        def square(n, h):
            a, b = span_of(square_spans(n), h)
            square_columns(n, a, 0, (b - a) * QT)

        def quantize_w(n, h=0):
            a = span_of(quantize_spans(n), h)[0]
            quantize(w_codes[n, a][:], w_scales[n, a][:], w_bf[n, a][:].rearrange("p n r -> p (n r)"))

        def y_matmul(qt, h, c):
            n = c * QTILES + qt
            a = span_of(quantize_spans(n), h)[0]
            queries = slice((h - a) * QT, (h - a + 1) * QT)
            nc.tensor.matmul_mx(
                out=y_bank(qt, h)[:, h, :],
                lhsT=w_codes[n, a][:, queries].bitcast(FP8X4),
                lhsT_scale=w_scales[n, a][:, queries],
                rhs=v_codes[c][:, h * D : (h + 1) * D].bitcast(FP8X4),
                rhs_scale=v_scales[c][:, h * D : (h + 1) * D],
                start=(c == 0),
                stop=(c == PASSES - 1),
            )

        def y_product(qt, h0, h1):
            for h in range(h0, h1):
                for c in range(PASSES):
                    y_matmul(qt, h, c)

        den, inv = {}, {}

        def denominators(qt, h0, h1):
            den[qt, h0] = tile("den%d_%d" % (qt, h0), [P, h1 - h0], F32)
            nc.vector.tensor_scalar(
                out=den[qt, h0][:], in0=y_bank(qt, h0)[:, h0:h1, D - 1], scalar1=1.0, scalar2=None, op0=ALU.add
            )

        def invert(qt, h0, h1):
            inv[qt, h0] = tile("inv%d_%d" % (qt, h0), [P, h1 - h0], F32)
            nc.vector.reciprocal(out=inv[qt, h0][:], in_=den[qt, h0][:])

        def store(qt, h0, h1, res):
            nc.sync.dma_start(out=out[h0:h1, qt * QT : (qt + 1) * QT, :].rearrange("h q e -> q h e"), in_=res[:])

        def divide_scalar(qt, h0, h1):
            res = tile("res%d_%d" % (qt, h0), [P, h1 - h0, D], F32)
            for h in range(h0, h1):
                nc.scalar.activation(
                    out=res[:, h - h0, :],
                    in_=y_bank(qt, h)[:, h, :],
                    func=ACT.Copy,
                    scale=inv[qt, h0][:, h - h0 : h - h0 + 1],
                )
            store(qt, h0, h1, res)

        def divide_vector(qt, h0, h1):
            res = tile("res%d_%d" % (qt, h0), [P, h1 - h0, D], F32)
            nc.vector.tensor_tensor(
                out=res[:],
                in0=y_bank(qt, h0)[:, h0:h1, :],
                in1=inv[qt, h0][:].unsqueeze(2).to_broadcast([P, h1 - h0, D]),
                op=ALU.mult,
            )
            store(qt, h0, h1, res)

        nc.vector.scalar_tensor_tensor(out=t_abs[:], in0=t_sb[:], scalar=-1.0, in1=t_sb[:], op0=ALU.mult, op1=ALU.max)
        nc.vector.tensor_scalar(out=t_step[:], in0=t_sb[:], scalar1=0.0, scalar2=2.0, op0=ALU.is_ge, op1=ALU.mult)
        nc.scalar.activation(out=guess[:], in_=t_abs[:], func=ACT.Sqrt)
        nc.vector.tensor_scalar(out=t_sign[:], in0=t_step[:], scalar1=-1.0, scalar2=None, op0=ALU.add)
        nc.vector.reciprocal(out=inv_guess[:], in_=guess[:])
        nc.vector.scalar_tensor_tensor(
            out=half_quot[:], in0=t_abs[:], scalar=0.5, in1=inv_guess[:], op0=ALU.mult, op1=ALU.mult
        )
        nc.vector.scalar_tensor_tensor(
            out=t_root[:], in0=guess[:], scalar=0.5, in1=half_quot[:], op0=ALU.mult, op1=ALU.add
        )

        cast_k(nc.vector.tensor_copy, 0, 0, K_SPLIT)
        cast_k(nc.scalar.copy, 0, K_SPLIT, P)
        cast_q(nc.vector.tensor_copy, 0)
        quantize_k(0, 0, PACK // 2)
        quantize_q(0)
        quantize_k(0, PACK // 2, PACK)
        to_fill.extend([(0, h, list(range(PACK))) for h in range(H)])
        fill_banks(PACK)
        scale_mask_vector(0, 0, QT)
        scale_mask_scalar(0, QT, 2 * QT)
        cast_q(nc.scalar.copy, 1)

        def batch(b):
            if b == 0:
                quantize_q(2)
                quantized_steps.extend([2, 3])
                fill_banks(PACK // 2)
            if b == 1:
                quantize_w(0)
            if b == 2:
                quantize_k(1, 0, PACK)
                quantized_steps.extend(range(QTILES, STEPS))
                fill_banks(PACK)
                scale_mask_vector(1, 0, NQ)
            if b == 3:
                quantize_w(1)
            if b == 4:
                quantize_w(QTILES)
                y_product(0, 0, 2)
            if b > 0:
                quantize_v(b - 1)
            if b < len(v_parts):
                cast_v(b)

        scalar_extras = {
            1 * H + 1: lambda: scale_mask_scalar(0, 2 * QT, NQ),
            1 * H + 3: lambda: cast_k(nc.scalar.copy, 1, 0, P),
        }

        for slot in range(FIRST_BATCH + len(v_parts) * WINDOW + 1):
            n, h = divmod(slot, H)
            gate(n, h)
            if slot == 1:
                quantize_q(1)
                cast_q_gpsimd(2)
                quantized_steps.append(1)
                fill_banks(PACK)
            if slot >= FIRST_BATCH and (slot - FIRST_BATCH) % WINDOW == 0:
                batch((slot - FIRST_BATCH) // WINDOW)
            if slot in scalar_extras:
                scalar_extras[slot]()
            if h % 2 == 1:
                square(n, h)

        y_product(0, 2, H)
        quantize_w(2)
        gate(6, 1)
        square(6, 1)
        quantize_w(5)
        y_product(1, 0, 2)
        denominators(0, 0, H)
        gate(6, 2)
        invert(0, 0, H)
        y_product(1, 2, H)
        divide_scalar(0, 0, H)
        gate(6, 3)
        square(6, 3)
        quantize_w(3)
        gate(LAST, 0)
        denominators(1, 0, H)
        square(LAST, 0)
        gate(LAST, 1)
        invert(1, 0, H)
        square(LAST, 1)
        quantize_w(6)
        y_product(2, 0, H)
        y_matmul(3, 2, 0)
        divide_scalar(1, 0, H)
        y_matmul(3, 3, 0)
        gate(LAST, 2)
        square(LAST, 2)
        halves = [(0, QT // 2), (QT // 2, QT)]
        for q0, q1 in halves:
            gate_columns(LAST, 3, q0, q1)
        for q0, q1 in halves:
            square_columns(LAST, 3, q0, q1)
        denominators(2, 0, H)
        quantize_w(LAST, 0)
        y_product(3, 0, 2)
        invert(2, 0, H)
        divide_vector(2, 0, H)
        quantize_w(LAST, 2)
        y_matmul(3, 2, 1)
        denominators(3, 0, 2)
        quantize_w(LAST, 3)
        y_matmul(3, 3, 1)
        invert(3, 0, 2)
        denominators(3, 2, 3)
        divide_scalar(3, 0, 2)
        invert(3, 2, 3)
        denominators(3, 3, 4)
        divide_vector(3, 2, 3)
        invert(3, 3, 4)
        divide_vector(3, 3, 4)
